import numpy as np, ml_dtypes
CORES = [32,160,288,416,80,208,336,464]
N = 8
import mx_ref
NC, G = 128, 2
C = np.float32(0.0217)
BF = ml_dtypes.bfloat16
def cut(t, i, w=512):
    return t[:, w * i:w * i + w]
def tile(rs):
    return np.stack(rs, axis=2).reshape(128, -1).astype(BF)
def layer(w, X):
    out = []
    for i in range(G):
        for t in range(len(X)):
            p = mx_ref.matmul(mx_ref.quantize(cut(w, len(X) * i + t)), X[t])
            z = p if t == 0 else z + p
        out.append(z)
    return out
def act(Z):
    return [np.maximum(s * z, 0) * C for z in Z for s in (1, -1)]
def setup_inputs(rng):
    def f(*shape):
        return mx_ref.flush((rng.standard_normal(shape, dtype=np.float32) * np.exp2(rng.integers(-2, 3, shape[:-1] + (1,)))).astype(BF))
    return {"s": f(N, 128, 4 * NC), "x": f(N, 128, 4 * NC), "w": f(N, 128, 2 * G * 512), "v": f(N, 128, 512)}
def setup_inputs_blocks(rng):
    d = setup_inputs(rng)
    for k in ("s", "x", "v"): d[k] = mx_ref.spread(d[k], rng, 4)
    for k in ("w",): d[k] = mx_ref.spread(d[k], rng, 1)
    return d
def setup_inputs_wide(rng):
    d = setup_inputs(rng)
    for k in ("s", "x", "v"): d[k] = mx_ref.flush((d[k].astype(np.float32) * np.exp2(rng.integers(-6, 7, (N, 1, 1))).astype(np.float32)).astype(BF))
    return d
def setup_inputs_zeros(rng):
    d = setup_inputs(rng); v = d["x"].reshape(N, 128, -1, 4).copy()
    v[np.broadcast_to((rng.random((N, 1, v.shape[2], 1)) < 0.33), v.shape)] = 0
    d["x"] = v.reshape(d["x"].shape)
    return d
def reference(s, x, w, v):
    q = mx_ref.quantize(s[0])
    y = np.zeros((N, 128, NC), np.float32)
    for r in range(N):
        q = mx_ref.quantize(tile(act(layer(w[r], [q, mx_ref.quantize(x[r])]))))
        y[r] = mx_ref.matmul(mx_ref.quantize(v[r]), q)
    return {"y": y}

@@ -1,0 +1,125 @@
+import numpy as np
+from concourse.mybir import dt, AluOpType, ActivationFunctionType
+
+NC = 128
+TW = 4 * NC
+C = float(np.float32(0.0217))
+SEND_ENGINES = 8
+
+SCRATCH = {
+    "bs": ("sbuf", [128, TW], "bfloat16"),
+    "bx": ("sbuf", [128, TW], "bfloat16"),
+    "bw": ("sbuf", [128, 4 * TW], "bfloat16"),
+    "bv": ("sbuf", [128, TW], "bfloat16"),
+    "h": ("sbuf", [128, TW], "bfloat16"),
+    "qi": ("sbuf", [128, NC], "float8_e4m3fn_x4"), "qi_s": ("sbuf", [128, NC], "uint8"),
+    "qx": ("sbuf", [128, NC], "float8_e4m3fn_x4"), "qx_s": ("sbuf", [128, NC], "uint8"),
+    "qw": ("sbuf", [128, 4 * 128], "float8_e4m3fn_x4"), "qw_s": ("sbuf", [128, 4 * 128], "uint8"),
+    "qv": ("sbuf", [128, 128], "float8_e4m3fn_x4"), "qv_s": ("sbuf", [128, 128], "uint8"),
+    "qo": ("sbuf", [128, NC], "float8_e4m3fn_x4"), "qo_s": ("sbuf", [128, NC], "uint8"),
+    "ps": ("psum", [128, 3 * 512], "float32"),
+    "yb": ("sbuf", [128, NC], "float32"),
+}
+SEMAPHORES = ["ld_s", "ld_x", "ld_wa", "ld_wb", "ld_v",
+              "k_s", "k_x", "k_w0", "k_w1", "k_w2", "k_w3", "k_v",
+              "arr", "z0", "z1", "a0", "a1", "qdone", "yz", "yc", "st", "sent"]
+
+
+def _engines(mask, k):
+    e = [i for i in range(16) if (mask >> i) & 1]
+    return sum(1 << i for i in e[:k])
+
+
+def rank_program(g, core, T, topo):
+    r = T.rank_of(core)
+    if r is None:
+        return
+    n = len(T.cores)
+    S = T.sem
+    first, last = r == 0, r == n - 1
+    ve, te, sc, sy = g.vector, g.tensor, g.scalar, g.sync
+
+    def wq(k):
+        return T.qw[:, 128 * k:128 * k + 128], T.qw_s[:, 128 * k:128 * k + 128]
+
+    sy.dma_start(T.bw[:, 0:2 * TW], T.w[:, 0:2 * TW]).then_inc(S.ld_wa, 16)
+    sc.dma_start(T.bx[:], T.x[:]).then_inc(S.ld_x, 16)
+    if first:
+        sy.dma_start(T.bs[:], T.s[:]).then_inc(S.ld_s, 16)
+    sc.dma_start(T.bw[:, 2 * TW:4 * TW], T.w[:, 2 * TW:4 * TW]).then_inc(S.ld_wb, 16)
+    sy.dma_start(T.bv[:], T.v[:]).then_inc(S.ld_v, 16)
+
+    def quant_w(k):
+        c, s = wq(k)
+        ve.quantize_mx(c, s, T.bw[:, TW * k:TW * k + TW]).then_inc(S["k_w%d" % k], 1)
+
+    def quant_v():
+        ve.wait_ge(S.ld_v, 16)
+        ve.quantize_mx(T.qv[:], T.qv_s[:], T.bv[:]).then_inc(S.k_v, 1)
+
+    ve.wait_ge(S.ld_x, 16)
+    ve.quantize_mx(T.qx[:], T.qx_s[:], T.bx[:]).then_inc(S.k_x, 1)
+    ve.wait_ge(S.ld_wa, 16)
+    quant_w(1)
+    quant_w(0)
+    if first:
+        ve.wait_ge(S.ld_s, 16)
+        ve.quantize_mx(T.qi[:], T.qi_s[:], T.bs[:]).then_inc(S.k_s, 1)
+    ve.wait_ge(S.ld_wb, 16)
+    quant_w(3)
+    quant_w(2)
+    if not first:
+        quant_v()
+
+    z = [T.ps[:, 0:NC], T.ps[:, 512:512 + NC]]
+    te.wait_ge(S.k_x, 1)
+    te.wait_ge(S.k_w1, 1)
+    te.matmul_mx(z[0], *wq(1), T.qx[:], T.qx_s[:], True, False)
+    if first:
+        te.wait_ge(S.k_w0, 1)
+        te.wait_ge(S.k_s, 1)
+        te.matmul_mx(z[0], *wq(0), T.qi[:], T.qi_s[:], False, True).then_inc(S.z0, 1)
+        te.wait_ge(S.k_w3, 1)
+        te.matmul_mx(z[1], *wq(3), T.qx[:], T.qx_s[:], True, False)
+        te.wait_ge(S.k_w2, 1)
+        te.matmul_mx(z[1], *wq(2), T.qi[:], T.qi_s[:], False, True).then_inc(S.z1, 1)
+    else:
+        te.wait_ge(S.k_w3, 1)
+        te.matmul_mx(z[1], *wq(3), T.qx[:], T.qx_s[:], True, False)
+        te.wait_ge(S.k_w0, 1)
+        te.wait_ge(S.k_w2, 1)
+        te.wait_ge(S.arr, 2 * SEND_ENGINES)
+        te.matmul_mx(z[0], *wq(0), T.qi[:], T.qi_s[:], False, True).then_inc(S.z0, 1)
+        te.matmul_mx(z[1], *wq(2), T.qi[:], T.qi_s[:], False, True).then_inc(S.z1, 1)
+
+    sc.wait_ge(S.z0, 1)
+    sc.activation(T.h[:, 0:TW:4], z[0], ActivationFunctionType.Relu, scale=C).then_inc(S.a0, 1)
+    sc.activation(T.h[:, 1:TW:4], z[0], ActivationFunctionType.Relu, scale=-C).then_inc(S.a0, 1)
+    ve.wait_ge(S.z1, 1)
+    ve.tensor_scalar(T.h[:, 2:TW:4], z[1], C, 0.0, AluOpType.mult, AluOpType.max).then_inc(S.a1, 1)
+    ve.tensor_scalar(T.h[:, 3:TW:4], z[1], -C, 0.0, AluOpType.mult, AluOpType.max).then_inc(S.a1, 1)
+    ve.wait_ge(S.a0, 2)
+    ve.wait_ge(S.a1, 2)
+    ve.quantize_mx(T.qo[:], T.qo_s[:], T.h[:]).then_inc(S.qdone, 1)
+    if first:
+        quant_v()
+
+    if not last:
+        dst = T.cores[r + 1]
+        rid, pid = topo.addr(dst, core)
+        m = _engines(topo.mask(core, dst), SEND_ENGINES)
+        g.wait_ge(S.qdone, 1)
+        g.remote_dma(T.qi[:].bitcast(dt.uint8), T.qo[:].bitcast(dt.uint8), S.arr, S.sent, pid, rid, m)
+        g.remote_dma(T.qi_s[:], T.qo_s[:], S.arr, S.sent, pid, rid, m)
+
+    yp = T.ps[:, 1024:1024 + NC]
+    te.wait_ge(S.k_v, 1)
+    te.wait_ge(S.qdone, 1)
+    te.matmul_mx(yp, T.qv[:], T.qv_s[:], T.qo[:], T.qo_s[:], True, True).then_inc(S.yz, 1)
+    ve.wait_ge(S.yz, 1)
+    ve.tensor_copy(T.yb[:], yp).then_inc(S.yc, 1)
+    sy.wait_ge(S.yc, 1)
+    if not last:
+        sy.wait_ge(S.sent, 2 * SEND_ENGINES)
+    sy.dma_start(T.y[:], T.yb[:]).then_inc(S.st, 16)
+    sy.wait_ge(S.st, 16)

@@ -5,6 +5,7 @@ NC = 128
 TW = 4 * NC
 C = float(np.float32(0.0217))
 SEND_ENGINES = 8
+PLACE = [0, 1, 2, 6, 5, 4, 3, 7]
 
 SCRATCH = {
     "bs": ("sbuf", [128, TW], "bfloat16"),
@@ -13,8 +14,9 @@ SCRATCH = {
     "bv": ("sbuf", [128, TW], "bfloat16"),
     "h": ("sbuf", [128, TW], "bfloat16"),
     "qi": ("sbuf", [128, NC], "float8_e4m3fn_x4"), "qi_s": ("sbuf", [128, NC], "uint8"),
-    "qx": ("sbuf", [128, NC], "float8_e4m3fn_x4"), "qx_s": ("sbuf", [128, NC], "uint8"),
-    "qw": ("sbuf", [128, 4 * 128], "float8_e4m3fn_x4"), "qw_s": ("sbuf", [128, 4 * 128], "uint8"),
+    "qy": ("sbuf", [128, NC], "float8_e4m3fn_x4"), "qy_s": ("sbuf", [128, NC], "uint8"),
+    "qw": ("sbuf", [128, 5 * 128], "float8_e4m3fn_x4"), "qw_s": ("sbuf", [128, 5 * 128], "uint8"),
+    "lw": ("sbuf", [128, 5 * 128], "float8_e4m3fn_x4"), "lw_s": ("sbuf", [128, 5 * 128], "uint8"),
     "qv": ("sbuf", [128, 128], "float8_e4m3fn_x4"), "qv_s": ("sbuf", [128, 128], "uint8"),
     "qo": ("sbuf", [128, NC], "float8_e4m3fn_x4"), "qo_s": ("sbuf", [128, NC], "uint8"),
     "ps": ("psum", [128, 3 * 512], "float32"),
@@ -22,6 +24,7 @@ SCRATCH = {
 }
 SEMAPHORES = ["ld_s", "ld_x", "ld_wa", "ld_wb", "ld_v",
               "k_s", "k_x", "k_w0", "k_w1", "k_w2", "k_w3", "k_v",
+              "warr", "wsent", "yarr",
               "arr", "z0", "z1", "a0", "a1", "qdone", "yz", "yc", "st", "sent"]
 
 
@@ -31,16 +34,33 @@ def _engines(mask, k):
 
 
 def rank_program(g, core, T, topo):
-    r = T.rank_of(core)
-    if r is None:
+    c = T.rank_of(core)
+    if c is None:
         return
     n = len(T.cores)
     S = T.sem
-    first, last = r == 0, r == n - 1
+    lay = PLACE.index(c)
+    home = lay == c
+    first = lay == 0
     ve, te, sc, sy = g.vector, g.tensor, g.scalar, g.sync
+    E2 = 2 * SEND_ENGINES
 
-    def wq(k):
+    def own(k):
         return T.qw[:, 128 * k:128 * k + 128], T.qw_s[:, 128 * k:128 * k + 128]
+
+    def use(k):
+        if home:
+            return own(k)
+        return T.lw[:, 128 * k:128 * k + 128], T.lw_s[:, 128 * k:128 * k + 128]
+
+    def send(dst_rank, pairs, rsem, lsem):
+        dst = T.cores[dst_rank]
+        assert topo.may_write(core, dst)
+        rid, pid = topo.addr(dst, core)
+        m = _engines(topo.mask(core, dst), SEND_ENGINES)
+        (oc, ic), (os_, is_) = pairs
+        g.remote_dma(oc[:].bitcast(dt.uint8), ic[:].bitcast(dt.uint8), rsem, lsem, pid, rid, m)
+        g.remote_dma(os_[:], is_[:], rsem, lsem, pid, rid, m)
 
     sy.dma_start(T.bw[:, 0:2 * TW], T.w[:, 0:2 * TW]).then_inc(S.ld_wa, 16)
     sc.dma_start(T.bx[:], T.x[:]).then_inc(S.ld_x, 16)
@@ -50,15 +70,15 @@ def rank_program(g, core, T, topo):
     sy.dma_start(T.bv[:], T.v[:]).then_inc(S.ld_v, 16)
 
     def quant_w(k):
-        c, s = wq(k)
-        ve.quantize_mx(c, s, T.bw[:, TW * k:TW * k + TW]).then_inc(S["k_w%d" % k], 1)
+        cd, pl = own(k)
+        ve.quantize_mx(cd, pl, T.bw[:, TW * k:TW * k + TW]).then_inc(S["k_w%d" % k], 1)
 
     def quant_v():
         ve.wait_ge(S.ld_v, 16)
         ve.quantize_mx(T.qv[:], T.qv_s[:], T.bv[:]).then_inc(S.k_v, 1)
 
     ve.wait_ge(S.ld_x, 16)
-    ve.quantize_mx(T.qx[:], T.qx_s[:], T.bx[:]).then_inc(S.k_x, 1)
+    ve.quantize_mx(*own(4), T.bx[:]).then_inc(S.k_x, 1)
     ve.wait_ge(S.ld_wa, 16)
     quant_w(1)
     quant_w(0)
@@ -71,27 +91,61 @@ def rank_program(g, core, T, topo):
     if not first:
         quant_v()
 
+    if not home:
+        for name in ("k_x", "k_w0", "k_w1", "k_w2", "k_w3"):
+            g.wait_ge(S[name], 1)
+        assert topo.same_plane(core, T.cores[PLACE[c]])
+        send(PLACE[c], ((T.lw, T.qw), (T.lw_s, T.qw_s)), S.warr, S.wsent)
+
+    yp = T.ps[:, 1024:1024 + NC]
+    y_early = c + 1 < lay
+
+    def y_tensor():
+        te.wait_ge(S.k_v, 1)
+        if home:
+            te.wait_ge(S.qdone, 1)
+            src = (T.qo[:], T.qo_s[:])
+        elif c + 1 == lay:
+            src = (T.qi[:], T.qi_s[:])
+        else:
+            te.wait_ge(S.yarr, E2)
+            src = (T.qy[:], T.qy_s[:])
+        te.matmul_mx(yp, T.qv[:], T.qv_s[:], src[0], src[1], True, True).then_inc(S.yz, 1)
+
+    def y_vector():
+        ve.wait_ge(S.yz, 1)
+        ve.tensor_copy(T.yb[:], yp).then_inc(S.yc, 1)
+
     z = [T.ps[:, 0:NC], T.ps[:, 512:512 + NC]]
-    te.wait_ge(S.k_x, 1)
-    te.wait_ge(S.k_w1, 1)
-    te.matmul_mx(z[0], *wq(1), T.qx[:], T.qx_s[:], True, False)
+    if home:
+        te.wait_ge(S.k_x, 1)
+        te.wait_ge(S.k_w1, 1)
+    else:
+        te.wait_ge(S.warr, E2)
+    te.matmul_mx(z[0], *use(1), *use(4), True, False)
     if first:
         te.wait_ge(S.k_w0, 1)
         te.wait_ge(S.k_s, 1)
-        te.matmul_mx(z[0], *wq(0), T.qi[:], T.qi_s[:], False, True).then_inc(S.z0, 1)
+        te.matmul_mx(z[0], *use(0), T.qi[:], T.qi_s[:], False, True).then_inc(S.z0, 1)
         te.wait_ge(S.k_w3, 1)
-        te.matmul_mx(z[1], *wq(3), T.qx[:], T.qx_s[:], True, False)
+        te.matmul_mx(z[1], *use(3), *use(4), True, False)
         te.wait_ge(S.k_w2, 1)
-        te.matmul_mx(z[1], *wq(2), T.qi[:], T.qi_s[:], False, True).then_inc(S.z1, 1)
+        te.matmul_mx(z[1], *use(2), T.qi[:], T.qi_s[:], False, True).then_inc(S.z1, 1)
     else:
-        te.wait_ge(S.k_w3, 1)
-        te.matmul_mx(z[1], *wq(3), T.qx[:], T.qx_s[:], True, False)
-        te.wait_ge(S.k_w0, 1)
-        te.wait_ge(S.k_w2, 1)
-        te.wait_ge(S.arr, 2 * SEND_ENGINES)
-        te.matmul_mx(z[0], *wq(0), T.qi[:], T.qi_s[:], False, True).then_inc(S.z0, 1)
-        te.matmul_mx(z[1], *wq(2), T.qi[:], T.qi_s[:], False, True).then_inc(S.z1, 1)
+        if home:
+            te.wait_ge(S.k_w3, 1)
+        te.matmul_mx(z[1], *use(3), *use(4), True, False)
+        if home:
+            te.wait_ge(S.k_w0, 1)
+            te.wait_ge(S.k_w2, 1)
+        if y_early:
+            y_tensor()
+        te.wait_ge(S.arr, E2)
+        te.matmul_mx(z[0], *use(0), T.qi[:], T.qi_s[:], False, True).then_inc(S.z0, 1)
+        te.matmul_mx(z[1], *use(2), T.qi[:], T.qi_s[:], False, True).then_inc(S.z1, 1)
 
+    if y_early:
+        y_vector()
     sc.wait_ge(S.z0, 1)
     sc.activation(T.h[:, 0:TW:4], z[0], ActivationFunctionType.Relu, scale=C).then_inc(S.a0, 1)
     sc.activation(T.h[:, 1:TW:4], z[0], ActivationFunctionType.Relu, scale=-C).then_inc(S.a0, 1)
@@ -104,22 +158,24 @@ def rank_program(g, core, T, topo):
     if first:
         quant_v()
 
-    if not last:
-        dst = T.cores[r + 1]
-        rid, pid = topo.addr(dst, core)
-        m = _engines(topo.mask(core, dst), SEND_ENGINES)
-        g.wait_ge(S.qdone, 1)
-        g.remote_dma(T.qi[:].bitcast(dt.uint8), T.qo[:].bitcast(dt.uint8), S.arr, S.sent, pid, rid, m)
-        g.remote_dma(T.qi_s[:], T.qo_s[:], S.arr, S.sent, pid, rid, m)
+    left = 0
+    g.wait_ge(S.qdone, 1)
+    if lay + 1 < n:
+        send(PLACE[lay + 1], ((T.qi, T.qo), (T.qi_s, T.qo_s)), S.arr, S.sent)
+        left += E2
+    if not home and (lay + 1 == n or PLACE[lay + 1] != lay):
+        send(lay, ((T.qy, T.qo), (T.qy_s, T.qo_s)), S.yarr, S.sent)
+        left += E2
 
-    yp = T.ps[:, 1024:1024 + NC]
-    te.wait_ge(S.k_v, 1)
-    te.wait_ge(S.qdone, 1)
-    te.matmul_mx(yp, T.qv[:], T.qv_s[:], T.qo[:], T.qo_s[:], True, True).then_inc(S.yz, 1)
-    ve.wait_ge(S.yz, 1)
-    ve.tensor_copy(T.yb[:], yp).then_inc(S.yc, 1)
+    if not y_early:
+        y_tensor()
+        y_vector()
     sy.wait_ge(S.yc, 1)
-    if not last:
-        sy.wait_ge(S.sent, 2 * SEND_ENGINES)
+    if left and not y_early:
+        sy.wait_ge(S.sent, left)
     sy.dma_start(T.y[:], T.yb[:]).then_inc(S.st, 16)
     sy.wait_ge(S.st, 16)
+    if not home:
+        g.wait_ge(S.wsent, E2)
+    if left:
+        g.wait_ge(S.sent, left)

@@ -1,11 +1,14 @@
 import numpy as np
 from concourse.mybir import dt, AluOpType, ActivationFunctionType
 
+WORLD = 512
 NC = 128
 TW = 4 * NC
 C = float(np.float32(0.0217))
 SEND_ENGINES = 8
-PLACE = [0, 1, 2, 6, 5, 4, 3, 7]
+PLACE = [0, 1, 5, 4, 3, 6, 2, 7]
+RELAYED = [4, 1, 0]
+DIRECT = (2, 4)
 
 SCRATCH = {
     "bs": ("sbuf", [128, TW], "bfloat16"),
@@ -17,6 +20,7 @@ SCRATCH = {
     "qy": ("sbuf", [128, NC], "float8_e4m3fn_x4"), "qy_s": ("sbuf", [128, NC], "uint8"),
     "qw": ("sbuf", [128, 5 * 128], "float8_e4m3fn_x4"), "qw_s": ("sbuf", [128, 5 * 128], "uint8"),
     "lw": ("sbuf", [128, 5 * 128], "float8_e4m3fn_x4"), "lw_s": ("sbuf", [128, 5 * 128], "uint8"),
+    "rw": ("sbuf", [128, 128], "float8_e4m3fn_x4"), "rw_s": ("sbuf", [128, 128], "uint8"),
     "qv": ("sbuf", [128, 128], "float8_e4m3fn_x4"), "qv_s": ("sbuf", [128, 128], "uint8"),
     "qo": ("sbuf", [128, NC], "float8_e4m3fn_x4"), "qo_s": ("sbuf", [128, NC], "uint8"),
     "ps": ("psum", [128, 3 * 512], "float32"),
@@ -24,18 +28,68 @@ SCRATCH = {
 }
 SEMAPHORES = ["ld_s", "ld_x", "ld_wa", "ld_wb", "ld_v",
               "k_s", "k_x", "k_w0", "k_w1", "k_w2", "k_w3", "k_v",
-              "warr", "wsent", "yarr",
+              "warr", "wsent", "yarr", "harr", "harp", "hsent",
               "arr", "z0", "z1", "a0", "a1", "qdone", "yz", "yc", "st", "sent"]
+KSEM = ["k_w0", "k_w1", "k_w2", "k_w3", "k_x"]
 
 
 def _engines(mask, k):
     e = [i for i in range(16) if (mask >> i) & 1]
+    assert len(e) >= k
     return sum(1 << i for i in e[:k])
+
+
+def _crosses(topo, a, b):
+    return topo.rack(topo.host(a)) != topo.rack(topo.host(b))
+
+
+def _relays(topo, core):
+    here = [k for k in range(WORLD) if topo.host(k) == topo.host(core) and topo.chip(k) == topo.chip(core)]
+    mate = [m for m in range(WORLD) if topo.mates(core, m)][0]
+
+    def group(k):
+        return (topo.die(k), topo.may_write(k, mate))
+    seen, out = [group(core)], []
+    for k in here:
+        if group(k) not in seen:
+            seen.append(group(k))
+            out.append(k)
+    return out
+
+
+def _write(g, topo, core, dst, pairs, rsems, lsem, m):
+    assert topo.may_write(core, dst)
+    rid, pid = topo.addr(dst, core)
+    (oc, ic), (os_, is_) = pairs
+    g.remote_dma(oc.bitcast(dt.uint8), ic.bitcast(dt.uint8), rsems[0], lsem, pid, rid, m)
+    g.remote_dma(os_, is_, rsems[1], lsem, pid, rid, m)
+
+
+def _relay_program(g, core, T, topo):
+    S = T.sem
+    for r, src in enumerate(T.cores):
+        dst = T.cores[PLACE[r]]
+        if PLACE[r] == r or not _crosses(topo, src, dst):
+            continue
+        rel = _relays(topo, src)[:len(RELAYED)]
+        if core not in rel:
+            continue
+        k = RELAYED[rel.index(core)]
+        assert topo.may_write(core, dst)
+        rid, pid = topo.addr(dst, core)
+        m = _engines(topo.mask(core, dst), SEND_ENGINES)
+        a, b = 128 * k, 128 * k + 128
+        g.wait_ge(S.harr, SEND_ENGINES)
+        g.remote_dma(T.lw[:, a:b].bitcast(dt.uint8), T.rw[:].bitcast(dt.uint8), S.warr, S.hsent, pid, rid, m)
+        g.wait_ge(S.harp, SEND_ENGINES)
+        g.remote_dma(T.lw_s[:, a:b], T.rw_s[:], S.warr, S.hsent, pid, rid, m)
+        g.wait_ge(S.hsent, 2 * SEND_ENGINES)
 
 
 def rank_program(g, core, T, topo):
     c = T.rank_of(core)
     if c is None:
+        _relay_program(g, core, T, topo)
         return
     n = len(T.cores)
     S = T.sem
@@ -45,8 +99,9 @@ def rank_program(g, core, T, topo):
     ve, te, sc, sy = g.vector, g.tensor, g.scalar, g.sync
     E2 = 2 * SEND_ENGINES
 
-    def own(k):
-        return T.qw[:, 128 * k:128 * k + 128], T.qw_s[:, 128 * k:128 * k + 128]
+    def own(k, k2=None):
+        e = 128 * (k + 1 if k2 is None else k2)
+        return T.qw[:, 128 * k:e], T.qw_s[:, 128 * k:e]
 
     def use(k):
         if home:
@@ -55,12 +110,7 @@ def rank_program(g, core, T, topo):
 
     def send(dst_rank, pairs, rsem, lsem):
         dst = T.cores[dst_rank]
-        assert topo.may_write(core, dst)
-        rid, pid = topo.addr(dst, core)
-        m = _engines(topo.mask(core, dst), SEND_ENGINES)
-        (oc, ic), (os_, is_) = pairs
-        g.remote_dma(oc[:].bitcast(dt.uint8), ic[:].bitcast(dt.uint8), rsem, lsem, pid, rid, m)
-        g.remote_dma(os_[:], is_[:], rsem, lsem, pid, rid, m)
+        _write(g, topo, core, dst, pairs, (rsem, rsem), lsem, _engines(topo.mask(core, dst), SEND_ENGINES))
 
     sy.dma_start(T.bw[:, 0:2 * TW], T.w[:, 0:2 * TW]).then_inc(S.ld_wa, 16)
     sc.dma_start(T.bx[:], T.x[:]).then_inc(S.ld_x, 16)
@@ -71,7 +121,7 @@ def rank_program(g, core, T, topo):
 
     def quant_w(k):
         cd, pl = own(k)
-        ve.quantize_mx(cd, pl, T.bw[:, TW * k:TW * k + TW]).then_inc(S["k_w%d" % k], 1)
+        ve.quantize_mx(cd, pl, T.bw[:, TW * k:TW * k + TW]).then_inc(S[KSEM[k]], 1)
 
     def quant_v():
         ve.wait_ge(S.ld_v, 16)
@@ -91,11 +141,29 @@ def rank_program(g, core, T, topo):
     if not first:
         quant_v()
 
+    wleft = 0
     if not home:
-        for name in ("k_x", "k_w0", "k_w1", "k_w2", "k_w3"):
-            g.wait_ge(S[name], 1)
-        assert topo.same_plane(core, T.cores[PLACE[c]])
-        send(PLACE[c], ((T.lw, T.qw), (T.lw_s, T.qw_s)), S.warr, S.wsent)
+        wdst = T.cores[PLACE[c]]
+        if _crosses(topo, core, wdst):
+            for hcore, k in zip(_relays(topo, core), RELAYED):
+                g.wait_ge(S[KSEM[k]], 1)
+                m = _engines(topo.mask(core, hcore) & ~topo.mask(core, wdst), SEND_ENGINES)
+                cd, pl = own(k)
+                _write(g, topo, core, hcore, ((T.rw[:], cd), (T.rw_s[:], pl)), (S.harr, S.harp), S.wsent, m)
+                wleft += E2
+            for k in range(*DIRECT):
+                g.wait_ge(S[KSEM[k]], 1)
+            cd, pl = own(*DIRECT)
+            a, b = 128 * DIRECT[0], 128 * DIRECT[1]
+            send(PLACE[c], ((T.lw[:, a:b], cd), (T.lw_s[:, a:b], pl)), S.warr, S.wsent)
+            wleft += E2
+        else:
+            for name in KSEM:
+                g.wait_ge(S[name], 1)
+            assert topo.same_plane(core, wdst)
+            send(PLACE[c], ((T.lw[:], T.qw[:]), (T.lw_s[:], T.qw_s[:])), S.warr, S.wsent)
+            wleft += E2
+    wexp = E2 * (1 + len(RELAYED)) if _crosses(topo, T.cores[lay], core) else E2
 
     yp = T.ps[:, 1024:1024 + NC]
     y_early = c + 1 < lay
@@ -121,7 +189,7 @@ def rank_program(g, core, T, topo):
         te.wait_ge(S.k_x, 1)
         te.wait_ge(S.k_w1, 1)
     else:
-        te.wait_ge(S.warr, E2)
+        te.wait_ge(S.warr, wexp)
     te.matmul_mx(z[0], *use(1), *use(4), True, False)
     if first:
         te.wait_ge(S.k_w0, 1)
@@ -161,10 +229,10 @@ def rank_program(g, core, T, topo):
     left = 0
     g.wait_ge(S.qdone, 1)
     if lay + 1 < n:
-        send(PLACE[lay + 1], ((T.qi, T.qo), (T.qi_s, T.qo_s)), S.arr, S.sent)
+        send(PLACE[lay + 1], ((T.qi[:], T.qo[:]), (T.qi_s[:], T.qo_s[:])), S.arr, S.sent)
         left += E2
     if not home and (lay + 1 == n or PLACE[lay + 1] != lay):
-        send(lay, ((T.qy, T.qo), (T.qy_s, T.qo_s)), S.yarr, S.sent)
+        send(lay, ((T.qy[:], T.qo[:]), (T.qy_s[:], T.qo_s[:])), S.yarr, S.sent)
         left += E2
 
     if not y_early:
@@ -175,7 +243,7 @@ def rank_program(g, core, T, topo):
         sy.wait_ge(S.sent, left)
     sy.dma_start(T.y[:], T.yb[:]).then_inc(S.st, 16)
     sy.wait_ge(S.st, 16)
-    if not home:
-        g.wait_ge(S.wsent, E2)
+    if wleft:
+        g.wait_ge(S.wsent, wleft)
     if left:
         g.wait_ge(S.sent, left)

import numpy as np
from concourse.mybir import dt, AluOpType, ActivationFunctionType

WORLD = 512
NC = 128
TW = 4 * NC
C = float(np.float32(0.0217))
SEND_ENGINES = 8
PLACE = [0, 1, 5, 4, 3, 6, 2, 7]
RELAYED = [4, 1, 0]
DIRECT = (2, 4)

SCRATCH = {
    "bs": ("sbuf", [128, TW], "bfloat16"),
    "bx": ("sbuf", [128, TW], "bfloat16"),
    "bw": ("sbuf", [128, 4 * TW], "bfloat16"),
    "bv": ("sbuf", [128, TW], "bfloat16"),
    "h": ("sbuf", [128, TW], "bfloat16"),
    "qi": ("sbuf", [128, NC], "float8_e4m3fn_x4"), "qi_s": ("sbuf", [128, NC], "uint8"),
    "qy": ("sbuf", [128, NC], "float8_e4m3fn_x4"), "qy_s": ("sbuf", [128, NC], "uint8"),
    "qw": ("sbuf", [128, 5 * 128], "float8_e4m3fn_x4"), "qw_s": ("sbuf", [128, 5 * 128], "uint8"),
    "lw": ("sbuf", [128, 5 * 128], "float8_e4m3fn_x4"), "lw_s": ("sbuf", [128, 5 * 128], "uint8"),
    "rw": ("sbuf", [128, 128], "float8_e4m3fn_x4"), "rw_s": ("sbuf", [128, 128], "uint8"),
    "qv": ("sbuf", [128, 128], "float8_e4m3fn_x4"), "qv_s": ("sbuf", [128, 128], "uint8"),
    "qo": ("sbuf", [128, NC], "float8_e4m3fn_x4"), "qo_s": ("sbuf", [128, NC], "uint8"),
    "ps": ("psum", [128, 3 * 512], "float32"),
    "yb": ("sbuf", [128, NC], "float32"),
}
SEMAPHORES = ["ld_s", "ld_x", "ld_wa", "ld_wb", "ld_v",
              "k_s", "k_x", "k_w0", "k_w1", "k_w2", "k_w3", "k_v",
              "warr", "wsent", "yarr", "harr", "harp", "hsent",
              "arr", "z0", "z1", "a0", "a1", "qdone", "yz", "yc", "st", "sent"]
KSEM = ["k_w0", "k_w1", "k_w2", "k_w3", "k_x"]


def _engines(mask, k):
    e = [i for i in range(16) if (mask >> i) & 1]
    assert len(e) >= k
    return sum(1 << i for i in e[:k])


def _crosses(topo, a, b):
    return topo.rack(topo.host(a)) != topo.rack(topo.host(b))


def _relays(topo, core):
    here = [k for k in range(WORLD) if topo.host(k) == topo.host(core) and topo.chip(k) == topo.chip(core)]
    mate = [m for m in range(WORLD) if topo.mates(core, m)][0]

    def group(k):
        return (topo.die(k), topo.may_write(k, mate))
    seen, out = [group(core)], []
    for k in here:
        if group(k) not in seen:
            seen.append(group(k))
            out.append(k)
    return out


def _write(g, topo, core, dst, pairs, rsems, lsem, m):
    assert topo.may_write(core, dst)
    rid, pid = topo.addr(dst, core)
    (oc, ic), (os_, is_) = pairs
    g.remote_dma(oc.bitcast(dt.uint8), ic.bitcast(dt.uint8), rsems[0], lsem, pid, rid, m)
    g.remote_dma(os_, is_, rsems[1], lsem, pid, rid, m)


def _relay_program(g, core, T, topo):
    S = T.sem
    for r, src in enumerate(T.cores):
        dst = T.cores[PLACE[r]]
        if PLACE[r] == r or not _crosses(topo, src, dst):
            continue
        rel = _relays(topo, src)[:len(RELAYED)]
        if core not in rel:
            continue
        k = RELAYED[rel.index(core)]
        assert topo.may_write(core, dst)
        rid, pid = topo.addr(dst, core)
        m = _engines(topo.mask(core, dst), SEND_ENGINES)
        a, b = 128 * k, 128 * k + 128
        g.wait_ge(S.harr, SEND_ENGINES)
        g.remote_dma(T.lw[:, a:b].bitcast(dt.uint8), T.rw[:].bitcast(dt.uint8), S.warr, S.hsent, pid, rid, m)
        g.wait_ge(S.harp, SEND_ENGINES)
        g.remote_dma(T.lw_s[:, a:b], T.rw_s[:], S.warr, S.hsent, pid, rid, m)
        g.wait_ge(S.hsent, 2 * SEND_ENGINES)


def rank_program(g, core, T, topo):
    c = T.rank_of(core)
    if c is None:
        _relay_program(g, core, T, topo)
        return
    n = len(T.cores)
    S = T.sem
    lay = PLACE.index(c)
    home = lay == c
    first = lay == 0
    ve, te, sc, sy = g.vector, g.tensor, g.scalar, g.sync
    E2 = 2 * SEND_ENGINES

    def own(k, k2=None):
        e = 128 * (k + 1 if k2 is None else k2)
        return T.qw[:, 128 * k:e], T.qw_s[:, 128 * k:e]

    def use(k):
        if home:
            return own(k)
        return T.lw[:, 128 * k:128 * k + 128], T.lw_s[:, 128 * k:128 * k + 128]

    def send(dst_rank, pairs, rsem, lsem):
        dst = T.cores[dst_rank]
        _write(g, topo, core, dst, pairs, (rsem, rsem), lsem, _engines(topo.mask(core, dst), SEND_ENGINES))

    sy.dma_start(T.bw[:, 0:2 * TW], T.w[:, 0:2 * TW]).then_inc(S.ld_wa, 16)
    sc.dma_start(T.bx[:], T.x[:]).then_inc(S.ld_x, 16)
    if first:
        sy.dma_start(T.bs[:], T.s[:]).then_inc(S.ld_s, 16)
    sc.dma_start(T.bw[:, 2 * TW:4 * TW], T.w[:, 2 * TW:4 * TW]).then_inc(S.ld_wb, 16)
    sy.dma_start(T.bv[:], T.v[:]).then_inc(S.ld_v, 16)

    def quant_w(k):
        cd, pl = own(k)
        ve.quantize_mx(cd, pl, T.bw[:, TW * k:TW * k + TW]).then_inc(S[KSEM[k]], 1)

    def quant_v():
        ve.wait_ge(S.ld_v, 16)
        ve.quantize_mx(T.qv[:], T.qv_s[:], T.bv[:]).then_inc(S.k_v, 1)

    ve.wait_ge(S.ld_x, 16)
    ve.quantize_mx(*own(4), T.bx[:]).then_inc(S.k_x, 1)
    ve.wait_ge(S.ld_wa, 16)
    quant_w(1)
    quant_w(0)
    if first:
        ve.wait_ge(S.ld_s, 16)
        ve.quantize_mx(T.qi[:], T.qi_s[:], T.bs[:]).then_inc(S.k_s, 1)
    ve.wait_ge(S.ld_wb, 16)
    quant_w(3)
    quant_w(2)
    if not first:
        quant_v()

    wleft = 0
    if not home:
        wdst = T.cores[PLACE[c]]
        if _crosses(topo, core, wdst):
            for hcore, k in zip(_relays(topo, core), RELAYED):
                g.wait_ge(S[KSEM[k]], 1)
                m = _engines(topo.mask(core, hcore) & ~topo.mask(core, wdst), SEND_ENGINES)
                cd, pl = own(k)
                _write(g, topo, core, hcore, ((T.rw[:], cd), (T.rw_s[:], pl)), (S.harr, S.harp), S.wsent, m)
                wleft += E2
            for k in range(*DIRECT):
                g.wait_ge(S[KSEM[k]], 1)
            cd, pl = own(*DIRECT)
            a, b = 128 * DIRECT[0], 128 * DIRECT[1]
            send(PLACE[c], ((T.lw[:, a:b], cd), (T.lw_s[:, a:b], pl)), S.warr, S.wsent)
            wleft += E2
        else:
            for name in KSEM:
                g.wait_ge(S[name], 1)
            assert topo.same_plane(core, wdst)
            send(PLACE[c], ((T.lw[:], T.qw[:]), (T.lw_s[:], T.qw_s[:])), S.warr, S.wsent)
            wleft += E2
    wexp = E2 * (1 + len(RELAYED)) if _crosses(topo, T.cores[lay], core) else E2

    yp = T.ps[:, 1024:1024 + NC]
    y_early = c + 1 < lay

    def y_tensor():
        te.wait_ge(S.k_v, 1)
        if home:
            te.wait_ge(S.qdone, 1)
            src = (T.qo[:], T.qo_s[:])
        elif c + 1 == lay:
            src = (T.qi[:], T.qi_s[:])
        else:
            te.wait_ge(S.yarr, E2)
            src = (T.qy[:], T.qy_s[:])
        te.matmul_mx(yp, T.qv[:], T.qv_s[:], src[0], src[1], True, True).then_inc(S.yz, 1)

    def y_vector():
        ve.wait_ge(S.yz, 1)
        ve.tensor_copy(T.yb[:], yp).then_inc(S.yc, 1)

    z = [T.ps[:, 0:NC], T.ps[:, 512:512 + NC]]
    if home:
        te.wait_ge(S.k_x, 1)
        te.wait_ge(S.k_w1, 1)
    else:
        te.wait_ge(S.warr, wexp)
    te.matmul_mx(z[0], *use(1), *use(4), True, False)
    if first:
        te.wait_ge(S.k_w0, 1)
        te.wait_ge(S.k_s, 1)
        te.matmul_mx(z[0], *use(0), T.qi[:], T.qi_s[:], False, True).then_inc(S.z0, 1)
        te.wait_ge(S.k_w3, 1)
        te.matmul_mx(z[1], *use(3), *use(4), True, False)
        te.wait_ge(S.k_w2, 1)
        te.matmul_mx(z[1], *use(2), T.qi[:], T.qi_s[:], False, True).then_inc(S.z1, 1)
    else:
        if home:
            te.wait_ge(S.k_w3, 1)
        te.matmul_mx(z[1], *use(3), *use(4), True, False)
        if home:
            te.wait_ge(S.k_w0, 1)
            te.wait_ge(S.k_w2, 1)
        if y_early:
            y_tensor()
        te.wait_ge(S.arr, E2)
        te.matmul_mx(z[0], *use(0), T.qi[:], T.qi_s[:], False, True).then_inc(S.z0, 1)
        te.matmul_mx(z[1], *use(2), T.qi[:], T.qi_s[:], False, True).then_inc(S.z1, 1)

    if y_early:
        y_vector()
    sc.wait_ge(S.z0, 1)
    sc.activation(T.h[:, 0:TW:4], z[0], ActivationFunctionType.Relu, scale=C).then_inc(S.a0, 1)
    sc.activation(T.h[:, 1:TW:4], z[0], ActivationFunctionType.Relu, scale=-C).then_inc(S.a0, 1)
    ve.wait_ge(S.z1, 1)
    ve.tensor_scalar(T.h[:, 2:TW:4], z[1], C, 0.0, AluOpType.mult, AluOpType.max).then_inc(S.a1, 1)
    ve.tensor_scalar(T.h[:, 3:TW:4], z[1], -C, 0.0, AluOpType.mult, AluOpType.max).then_inc(S.a1, 1)
    ve.wait_ge(S.a0, 2)
    ve.wait_ge(S.a1, 2)
    ve.quantize_mx(T.qo[:], T.qo_s[:], T.h[:]).then_inc(S.qdone, 1)
    if first:
        quant_v()

    left = 0
    g.wait_ge(S.qdone, 1)
    if lay + 1 < n:
        send(PLACE[lay + 1], ((T.qi[:], T.qo[:]), (T.qi_s[:], T.qo_s[:])), S.arr, S.sent)
        left += E2
    if not home and (lay + 1 == n or PLACE[lay + 1] != lay):
        send(lay, ((T.qy[:], T.qo[:]), (T.qy_s[:], T.qo_s[:])), S.yarr, S.sent)
        left += E2

    if not y_early:
        y_tensor()
        y_vector()
    sy.wait_ge(S.yc, 1)
    if left and not y_early:
        sy.wait_ge(S.sent, left)
    sy.dma_start(T.y[:], T.yb[:]).then_inc(S.st, 16)
    sy.wait_ge(S.st, 16)
    if wleft:
        g.wait_ge(S.wsent, wleft)
    if left:
        g.wait_ge(S.sent, left)
